import numpy as np
import ml_dtypes


def mxq(x, axis, fmt="e4m3"):
    dtype, down = {"e4m3": (ml_dtypes.float8_e4m3fn, 7), "e5m2": (ml_dtypes.float8_e5m2, 14)}[fmt]
    v = np.moveaxis(np.asarray(x, np.float32).astype(ml_dtypes.bfloat16).astype(np.float64), axis, -1)
    blocks = v.reshape(v.shape[:-1] + (-1, 32))
    amax = np.abs(blocks).max(-1, keepdims=True)
    byte = np.maximum(np.where(amax > 0, np.frexp(amax)[1] - 1 + 127, 0) - down, 1)
    scale = np.exp2(byte - 127.0)
    codes = (blocks / scale).astype(np.float32).astype(dtype).astype(np.float64)
    return np.moveaxis((codes * scale).reshape(v.shape), -1, axis)


WIDE = False


def mx_kscale(k):
    if not WIDE:
        return np.ones(k)
    levels = np.array([10, -10, 5, -5, 0])
    if k % 512:
        return np.exp2(np.random.permutation(np.resize(levels, k // 32))).repeat(32)
    a = np.empty((k // 512, 16))
    for p in range(k // 512):
        a[p, :8] = np.random.permutation(np.resize(levels, 8))
        for g in range(8):
            far = levels[np.abs(levels - a[p, g]) >= 10]
            a[p, g + 8] = far[np.random.randint(len(far))]
    return np.exp2(a.ravel()).repeat(32)


def f64(x):
    return np.asarray(x).astype(np.float64)


def striped(idx):
    return np.tile(np.asarray(idx).reshape(-1, 16).T, (8, 1)).astype(np.uint16)


def unstriped(offs):
    return offs[:16].T.reshape(-1).astype(np.int64)


E2M1 = np.array([0.0, 0.5, 1.0, 1.5, 2.0, 3.0, 4.0, 6.0, -0.0, -0.5, -1.0, -1.5, -2.0, -3.0, -4.0, -6.0])


def pack_weight(w, fmt):
    k, n = w.shape
    w = f64(np.asarray(w, np.float32).astype(ml_dtypes.bfloat16)).reshape(k // 32, 32, n)
    amax = np.abs(w).max(1)
    if fmt == "e4m3":
        byte = np.frexp(amax)[1] - 1 + 127 - 7
    else:
        mant, ex = np.frexp(amax / 6.0)
        byte = np.where(mant > 0.5, ex, ex - 1) + 127
    byte = np.clip(np.where(amax > 0, byte, 1), 1, 254)
    scaled = (w * np.exp2(127.0 - byte)[:, None, :]).reshape(k, n).astype(np.float32)
    by_word = np.ascontiguousarray(scaled.reshape(k // 512, 128, 4, n).transpose(0, 1, 3, 2))
    if fmt == "e4m3":
        words = by_word.astype(ml_dtypes.float8_e4m3fn).view(np.uint8)
    else:
        c = by_word.astype(ml_dtypes.float4_e2m1fn).view(np.uint8) & 0xF
        words = (c[..., 0::2] | (c[..., 1::2] << 4)).reshape(k // 512, 128, 2 * n)
    return np.ascontiguousarray(words), np.ascontiguousarray(byte.astype(np.uint8).reshape(k // 512, 16, n))


def unpack_weight(words, scales, fmt):
    g, _, n = scales.shape
    words = np.ascontiguousarray(words).reshape(g, 128, n, -1)
    if fmt == "e4m3":
        vals = words.view(ml_dtypes.float8_e4m3fn).astype(np.float64)
    else:
        nib = np.empty((g, 128, n, 4), np.uint8)
        nib[..., 0::2] = words & 0xF
        nib[..., 1::2] = words >> 4
        vals = E2M1[nib]
    vals = vals * np.repeat(np.exp2(scales.astype(np.float64) - 127.0), 8, axis=1)[..., None]
    return vals.transpose(0, 1, 3, 2).reshape(g * 512, n)


D, T, I, Q, U, G, M = 512, 2048, 512, 128, 1024, 64, 512


def setup_inputs():
    n = np.random.standard_normal
    idx = np.random.permutation(T)[:I]
    idx2 = np.random.permutation(U)[:I]
    idx3 = np.random.permutation(M)[:G]
    fd = mx_kscale(D)
    keysp = pack_weight(n((D, T)) / fd[:, None], "e4m3")
    return {
        "query": (n((D, Q)) * 0.7 / np.sqrt(D) * fd[:, None]).astype(np.float32),
        "query2": (n((D, Q)) * 0.7 / np.sqrt(D) * fd[:, None]).astype(np.float32),
        "keys_words": keysp[0],
        "keys_scales": keysp[1],
        "notes": (n((D, U)) / fd[:, None]).astype(np.float32),
        "worth": np.tile(np.random.uniform(0.2, 2.0, T), (128, 1)).astype(np.float32),
        "old": (1.0 * n((Q, M))).astype(np.float32),
        "offs": striped(idx),
        "offs2": striped(idx2),
        "offs3": striped(idx3),
    }


def reference(query, query2, keys_words, keys_scales, notes, worth, old, offs, offs2, offs3):
    idx = unstriped(offs)
    idx2 = unstriped(offs2)
    idx3 = unstriped(offs3)
    keysu = unpack_weight(keys_words, keys_scales, "e4m3")
    queryq = mxq(f64(query), 0, "e4m3")
    keysidxg = keysu[:, idx]
    query2q = mxq(f64(query2), 0, "e4m3")
    notesidx2q = mxq(f64(notes)[:, idx2], 0, "e4m3")
    s = queryq.T @ keysidxg + query2q.T @ notesidx2q
    w = np.maximum(s, 0.0)
    ws = w * f64(worth)[:1][:, idx] * 2.0
    wp = ws.reshape(Q, G, I // G).sum(axis=2)
    wf = np.zeros((Q, M))
    wf[:, idx3] = wp
    y = f64(old) + wf
    return y

@@ -1,0 +1,184 @@
+from contextlib import ExitStack
+
+import concourse.mybir as mybir
+from concourse.masks import make_identity
+
+D, T, I, Q, U, G, M = 512, 2048, 512, 128, 1024, 64, 512
+RUN = I // G
+
+FLOPS = 2 * 2 * D * Q * I
+BYTES = 2 * D * Q * 4 + D * T + 16 * T + D * U * 4 + T * 4 + 2 * Q * M * 4 + 128 * (32 + 32 + 4) * 2
+
+F32 = mybir.dt.float32
+BF16 = mybir.dt.bfloat16
+I32 = mybir.dt.int32
+U32 = mybir.dt.uint32
+U16 = mybir.dt.uint16
+U8 = mybir.dt.uint8
+FP8X4 = mybir.dt.float8_e4m3fn_x4
+ALU = mybir.AluOpType
+COPY = mybir.ActivationFunctionType.Copy
+
+P = 128
+PACK = 4
+HALF = I // 2
+WORTH_ROW = P - 1
+PIECES = ((0, 256), (256, 128), (384, 128))
+
+
+def weave_views(dst, src):
+    return (
+        dst.rearrange("p (c i) t -> p c t i", i=4),
+        src.rearrange("p t (c i) -> p c t i", i=4),
+    )
+
+
+def tile_attend_twosources_pagesums_lean_kernel(
+    tc, query, query2, keys_words, keys_scales, notes, worth, old, offs, offs2, offs3, out
+):
+    nc = tc.nc
+    with ExitStack() as ctx:
+        sb = ctx.enter_context(tc.tile_pool(name="sb", bufs=1))
+        ps = ctx.enter_context(tc.psum_pool(name="ps", bufs=1))
+
+        tok_list = sb.tile([P, I // 16], U16, name="tok_list")
+        note_list = sb.tile([P, I // 16], U16, name="note_list")
+        col_list = sb.tile([P, G // 16], U16, name="col_list")
+        key_scales = sb.tile([P, T], U8, name="key_scales", align_bytes=64)
+        key_words = sb.tile([P, T], I32, name="key_words", align_bytes=64)
+        worth_pool = sb.tile([P, T], F32, name="worth_pool")
+        planes = [sb.tile([P, U], F32, name=f"plane{t}") for t in range(PACK)]
+        q_raw = [sb.tile([P, PACK, Q], F32, name=f"q_raw{s}") for s in range(2)]
+        old_sb = sb.tile([P, M], F32, name="old_sb")
+        placed = sb.tile([P, M], F32, name="placed")
+        ident = sb.tile([P, P], F32, name="ident")
+
+        nc.gpsimd.memset(key_scales[:].bitcast(I32), 0)
+        nc.vector.memset(worth_pool[0:WORTH_ROW, :], 0.0)
+        make_identity(nc, ident[:])
+        nc.gpsimd.memset(placed[:], 0.0)
+
+        note_rows = notes.rearrange("(p t) u -> p t u", t=PACK)
+        scale_rows = keys_scales[0].bitcast(I32)
+        nc.sync.dma_start(note_list[:], offs2)
+        nc.sync.dma_start(planes[0][:], note_rows[:, 0, :])
+        nc.sync.dma_start(tok_list[:], offs)
+        nc.sync.dma_start(worth_pool[WORTH_ROW : WORTH_ROW + 1, :], worth[0:1, :])
+        for t in range(1, PACK):
+            nc.sync.dma_start(planes[t][:], note_rows[:, t, :])
+        nc.sync.dma_start(q_raw[0][:], query2.rearrange("(p t) q -> p t q", t=PACK))
+        for quad in range(4):
+            nc.scalar.dma_start(
+                key_scales[32 * quad : 32 * quad + 4, :].bitcast(I32), scale_rows[4 * quad : 4 * quad + 4, :]
+            )
+        nc.sync.dma_start(q_raw[1][:], query.rearrange("(p t) q -> p t q", t=PACK))
+        nc.sync.dma_start(key_words[:], keys_words[0].rearrange("p n t -> p (n t)").bitcast(I32))
+        nc.sync.dma_start(old_sb[:], old)
+        nc.sync.dma_start(col_list[:], offs3)
+
+        def half_list(lst, h):
+            return lst[:, h * (HALF // 16) : (h + 1) * (HALF // 16)]
+
+        picked = [sb.tile([P, PACK, HALF], BF16, name=f"picked{h}") for h in range(2)]
+
+        def gather_note(t, h, on_scalar):
+            src = planes[t][:].indirect(half_list(note_list, h))
+            if on_scalar:
+                nc.scalar.activation(picked[h][:, t, :], src, COPY)
+            else:
+                nc.vector.tensor_copy(picked[h][:, t, :], src)
+
+        worth_row = sb.tile([P, I], F32, name="worth_row")
+        k_scales = sb.tile([P, I], U8, name="k_scales", align_bytes=64)
+
+        nc.vector.tensor_copy(k_scales[:], key_scales[:].indirect(tok_list[:]))
+        gather_note(0, 0, False)
+        gather_note(0, 1, False)
+        nc.scalar.activation(worth_row[:], worth_pool[:].indirect(tok_list[:]), COPY)
+        gather_note(1, 0, True)
+        gather_note(1, 1, True)
+        gather_note(2, 0, False)
+        gather_note(2, 1, True)
+        gather_note(3, 0, False)
+        gather_note(3, 1, True)
+
+        woven = [sb.tile([P, HALF, PACK], BF16, name=f"woven{h}", align_bytes=64) for h in range(2)]
+        n_codes = [sb.tile([P, HALF], U32, name=f"n_codes{h}", align_bytes=64) for h in range(2)]
+        n_scales = [sb.tile([P, HALF], U8, name=f"n_scales{h}", align_bytes=64) for h in range(2)]
+        for h in range(2):
+            dst, src = weave_views(woven[h][:], picked[h][:])
+            nc.vector.tensor_copy(dst, src)
+        for h in range(2):
+            nc.vector.quantize_mx(
+                out=n_codes[h][:].bitcast(FP8X4),
+                scales=n_scales[h][:],
+                in_=woven[h][:].rearrange("p c t -> p (c t)"),
+            )
+
+        q_woven = sb.tile([P, 2 * Q, PACK], BF16, name="q_woven", align_bytes=64)
+        q_codes = sb.tile([P, 2 * Q], U32, name="q_codes", align_bytes=64)
+        q_scales = sb.tile([P, 2 * Q], U8, name="q_scales", align_bytes=64)
+        for s in range(2):
+            dst, src = weave_views(q_woven[:, s * Q : (s + 1) * Q, :], q_raw[s][:])
+            nc.scalar.copy(dst, src)
+        nc.vector.quantize_mx(
+            out=q_codes[:].bitcast(FP8X4), scales=q_scales[:], in_=q_woven[:].rearrange("p c t -> p (c t)")
+        )
+
+        turned = ps.tile([P, I // P, P], F32, name="turned")
+        spread = ps.tile([P, I], F32, name="spread")
+        worth_col = sb.tile([P, I // P], F32, name="worth_col")
+        weight = sb.tile([P, I], F32, name="weight")
+        for c in range(I // P):
+            nc.tensor.transpose(turned[:, c, :], worth_row[:, c * P : (c + 1) * P], ident[:])
+        nc.scalar.activation(worth_col[:], turned[:, :, WORTH_ROW], COPY, scale=2.0)
+        for c in range(I // P):
+            nc.tensor.transpose(
+                spread[:, c * P : (c + 1) * P], worth_col[:, c : c + 1].to_broadcast([P, P]), ident[:]
+            )
+        nc.scalar.copy(weight[:], spread[:])
+
+        k_codes = [sb.tile([P, n], U32, name=f"k_codes{lo}", align_bytes=64) for lo, n in PIECES]
+        scores = [ps.tile([P, n], F32, name=f"scores{lo}") for lo, n in PIECES]
+        for (lo, n), bank in zip(PIECES, scores):
+            h, at = divmod(lo, HALF)
+            nc.tensor.matmul_mx(
+                out=bank[:],
+                lhsT=q_codes[:, 0:Q].bitcast(FP8X4),
+                lhsT_scale=q_scales[:, 0:Q],
+                rhs=n_codes[h][:, at : at + n].bitcast(FP8X4),
+                rhs_scale=n_scales[h][:, at : at + n],
+                start=True,
+                stop=False,
+            )
+        for (lo, n), bank, codes in zip(PIECES, scores, k_codes):
+            nc.vector.tensor_copy(
+                codes[:], key_words[:].bitcast(U32).indirect(tok_list[:, lo // 16 : (lo + n) // 16])
+            )
+            nc.tensor.matmul_mx(
+                out=bank[:],
+                lhsT=q_codes[:, Q : 2 * Q].bitcast(FP8X4),
+                lhsT_scale=q_scales[:, Q : 2 * Q],
+                rhs=codes[:].bitcast(FP8X4),
+                rhs_scale=k_scales[:, lo : lo + n],
+                start=False,
+                stop=True,
+            )
+
+        weighted = [sb.tile([P, n], F32, name=f"weighted{lo}") for lo, n in PIECES]
+        sums = sb.tile([P, G], F32, name="sums")
+        for (lo, n), bank, ws in zip(PIECES, scores, weighted):
+            nc.vector.scalar_tensor_tensor(ws[:], bank[:], 0.0, weight[:, lo : lo + n], ALU.max, ALU.mult)
+        for (lo, n), ws in zip(PIECES, weighted):
+            nc.vector.tensor_reduce(
+                sums[:, lo // RUN : (lo + n) // RUN],
+                ws[:].rearrange("p (g j) -> p g j", j=RUN),
+                mybir.AxisListType.X,
+                ALU.add,
+            )
+        nc.scalar.activation(placed[:].indirect(col_list[:]), sums[:], COPY)
+        for h, queue in enumerate((nc.sync, nc.scalar)):
+            cols = slice(h * (M // 2), (h + 1) * (M // 2))
+            result = sb.tile([P, M // 2], F32, name=f"result{h}")
+            nc.vector.tensor_tensor(result[:], placed[:, cols], old_sb[:, cols], ALU.add)
+            queue.dma_start(out[:, cols], result[:])

@@ -53,6 +53,9 @@ def tile_attend_twosources_pagesums_lean_kernel(
         placed = sb.tile([P, M], F32, name="placed")
         ident = sb.tile([P, P], F32, name="ident")
 
+        warm = sb.tile([P, 2], F32, name="warm")
+        nc.gpsimd.memset(warm[:, 0:1], 0.0)
+        nc.scalar.activation(warm[:, 1:2], warm[:, 0:1], COPY)
         nc.gpsimd.memset(key_scales[:].bitcast(I32), 0)
         nc.vector.memset(worth_pool[0:WORTH_ROW, :], 0.0)
         make_identity(nc, ident[:])

@@ -23,6 +23,8 @@ P = 128
 PACK = 4
 HALF = I // 2
 WORTH_ROW = P - 1
+BLOCKS = D // 32
+SCALE_ROW = 64 - BLOCKS
 PIECES = ((0, 256), (256, 128), (384, 128))
 
 
@@ -47,42 +49,39 @@ def tile_attend_twosources_pagesums_lean_kernel(
         key_scales = sb.tile([P, T], U8, name="key_scales", align_bytes=64)
         key_words = sb.tile([P, T], I32, name="key_words", align_bytes=64)
         worth_pool = sb.tile([P, T], F32, name="worth_pool")
-        planes = [sb.tile([P, U], F32, name=f"plane{t}") for t in range(PACK)]
+        planes = [sb.tile([P, U], F32, name=f"plane{t}", tag=f"plane{t}") for t in range(PACK)]
         q_raw = [sb.tile([P, PACK, Q], F32, name=f"q_raw{s}") for s in range(2)]
-        old_sb = sb.tile([P, M], F32, name="old_sb")
         placed = sb.tile([P, M], F32, name="placed")
+        k_scales = sb.tile([P, I], U8, name="k_scales", align_bytes=64)
         ident = sb.tile([P, P], F32, name="ident")
 
         warm = sb.tile([P, 2], F32, name="warm")
         nc.gpsimd.memset(warm[:, 0:1], 0.0)
         nc.scalar.activation(warm[:, 1:2], warm[:, 0:1], COPY)
-        nc.gpsimd.memset(key_scales[:].bitcast(I32), 0)
+        nc.gpsimd.memset(key_scales[SCALE_ROW + BLOCKS :, :].bitcast(I32), 0)
         nc.vector.memset(worth_pool[0:WORTH_ROW, :], 0.0)
+        nc.vector.memset(key_scales[0:SCALE_ROW, :].bitcast(I32), 0)
         make_identity(nc, ident[:])
-        nc.gpsimd.memset(placed[:], 0.0)
+        nc.vector.memset(k_scales[:].bitcast(I32), 0)
 
         note_rows = notes.rearrange("(p t) u -> p t u", t=PACK)
         scale_rows = keys_scales[0].bitcast(I32)
-        nc.sync.dma_start(note_list[:], offs2)
         nc.sync.dma_start(planes[0][:], note_rows[:, 0, :])
+        nc.sync.dma_start(note_list[:], offs2)
         nc.sync.dma_start(tok_list[:], offs)
+        nc.sync.dma_start(key_scales[SCALE_ROW : SCALE_ROW + BLOCKS, :].bitcast(I32), scale_rows)
         nc.sync.dma_start(worth_pool[WORTH_ROW : WORTH_ROW + 1, :], worth[0:1, :])
         for t in range(1, PACK):
             nc.sync.dma_start(planes[t][:], note_rows[:, t, :])
         nc.sync.dma_start(q_raw[0][:], query2.rearrange("(p t) q -> p t q", t=PACK))
-        for quad in range(4):
-            nc.scalar.dma_start(
-                key_scales[32 * quad : 32 * quad + 4, :].bitcast(I32), scale_rows[4 * quad : 4 * quad + 4, :]
-            )
         nc.sync.dma_start(q_raw[1][:], query.rearrange("(p t) q -> p t q", t=PACK))
         nc.sync.dma_start(key_words[:], keys_words[0].rearrange("p n t -> p (n t)").bitcast(I32))
-        nc.sync.dma_start(old_sb[:], old)
         nc.sync.dma_start(col_list[:], offs3)
 
         def half_list(lst, h):
             return lst[:, h * (HALF // 16) : (h + 1) * (HALF // 16)]
 
-        picked = [sb.tile([P, PACK, HALF], BF16, name=f"picked{h}") for h in range(2)]
+        picked = [sb.tile([P, PACK, HALF], BF16, name=f"picked{h}", tag=f"staging{h}") for h in range(2)]
 
         def gather_note(t, h, on_scalar):
             src = planes[t][:].indirect(half_list(note_list, h))
@@ -92,18 +91,26 @@ def tile_attend_twosources_pagesums_lean_kernel(
                 nc.vector.tensor_copy(picked[h][:, t, :], src)
 
         worth_row = sb.tile([P, I], F32, name="worth_row")
-        k_scales = sb.tile([P, I], U8, name="k_scales", align_bytes=64)
+        picked_scales = sb.tile([P, I], U8, name="picked_scales", align_bytes=64)
 
-        nc.vector.tensor_copy(k_scales[:], key_scales[:].indirect(tok_list[:]))
         gather_note(0, 0, False)
         gather_note(0, 1, False)
+        nc.vector.tensor_copy(picked_scales[:], key_scales[:].indirect(tok_list[:]))
+        for quad in range(4):
+            row = SCALE_ROW + 4 * quad
+            nc.sync.dma_start(
+                k_scales[32 * quad : 32 * quad + 4, :].bitcast(I32), picked_scales[row : row + 4, :].bitcast(I32)
+            )
         nc.scalar.activation(worth_row[:], worth_pool[:].indirect(tok_list[:]), COPY)
         gather_note(1, 0, True)
         gather_note(1, 1, True)
         gather_note(2, 0, False)
         gather_note(2, 1, True)
+        nc.vector.memset(placed[:], 0.0)
         gather_note(3, 0, False)
         gather_note(3, 1, True)
+        old_sb = sb.tile([P, M], F32, name="old_sb", tag="plane3")
+        nc.sync.dma_start(old_sb[:], old)
 
         woven = [sb.tile([P, HALF, PACK], BF16, name=f"woven{h}", align_bytes=64) for h in range(2)]
         n_codes = [sb.tile([P, HALF], U32, name=f"n_codes{h}", align_bytes=64) for h in range(2)]
@@ -131,7 +138,7 @@ def tile_attend_twosources_pagesums_lean_kernel(
         turned = ps.tile([P, I // P, P], F32, name="turned")
         spread = ps.tile([P, I], F32, name="spread")
         worth_col = sb.tile([P, I // P], F32, name="worth_col")
-        weight = sb.tile([P, I], F32, name="weight")
+        weight = sb.tile([P, I], F32, name="weight", tag="staging1")
         for c in range(I // P):
             nc.tensor.transpose(turned[:, c, :], worth_row[:, c * P : (c + 1) * P], ident[:])
         nc.scalar.activation(worth_col[:], turned[:, :, WORTH_ROW], COPY, scale=2.0)

@@ -23,6 +23,7 @@ P = 128
 PACK = 4
 HALF = I // 2
 WORTH_ROW = P - 1
+WEAVE_SPLIT = 160
 BLOCKS = D // 32
 SCALE_ROW = 64 - BLOCKS
 PIECES = ((0, 256), (256, 128), (384, 128))
@@ -115,9 +116,9 @@ def tile_attend_twosources_pagesums_lean_kernel(
         woven = [sb.tile([P, HALF, PACK], BF16, name=f"woven{h}", align_bytes=64) for h in range(2)]
         n_codes = [sb.tile([P, HALF], U32, name=f"n_codes{h}", align_bytes=64) for h in range(2)]
         n_scales = [sb.tile([P, HALF], U8, name=f"n_scales{h}", align_bytes=64) for h in range(2)]
-        for h in range(2):
-            dst, src = weave_views(woven[h][:], picked[h][:])
-            nc.vector.tensor_copy(dst, src)
+        nc.vector.tensor_copy(*weave_views(woven[0][:], picked[0][:]))
+        nc.vector.tensor_copy(*weave_views(woven[1][:, :WEAVE_SPLIT, :], picked[1][:, :, :WEAVE_SPLIT]))
+        nc.scalar.copy(*weave_views(woven[1][:, WEAVE_SPLIT:, :], picked[1][:, :, WEAVE_SPLIT:]))
         for h in range(2):
             nc.vector.quantize_mx(
                 out=n_codes[h][:].bitcast(FP8X4),

from contextlib import ExitStack

import concourse.mybir as mybir
from concourse.masks import make_identity

D, T, I, Q, U, G, M = 512, 2048, 512, 128, 1024, 64, 512
RUN = I // G

FLOPS = 2 * 2 * D * Q * I
BYTES = 2 * D * Q * 4 + D * T + 16 * T + D * U * 4 + T * 4 + 2 * Q * M * 4 + 128 * (32 + 32 + 4) * 2

F32 = mybir.dt.float32
BF16 = mybir.dt.bfloat16
I32 = mybir.dt.int32
U32 = mybir.dt.uint32
U16 = mybir.dt.uint16
U8 = mybir.dt.uint8
FP8X4 = mybir.dt.float8_e4m3fn_x4
ALU = mybir.AluOpType
COPY = mybir.ActivationFunctionType.Copy

P = 128
PACK = 4
HALF = I // 2
WORTH_ROW = P - 1
WEAVE_SPLIT = 160
BLOCKS = D // 32
SCALE_ROW = 64 - BLOCKS
PIECES = ((0, 256), (256, 128), (384, 128))


def weave_views(dst, src):
    return (
        dst.rearrange("p (c i) t -> p c t i", i=4),
        src.rearrange("p t (c i) -> p c t i", i=4),
    )


def tile_attend_twosources_pagesums_lean_kernel(
    tc, query, query2, keys_words, keys_scales, notes, worth, old, offs, offs2, offs3, out
):
    nc = tc.nc
    with ExitStack() as ctx:
        sb = ctx.enter_context(tc.tile_pool(name="sb", bufs=1))
        ps = ctx.enter_context(tc.psum_pool(name="ps", bufs=1))

        tok_list = sb.tile([P, I // 16], U16, name="tok_list")
        note_list = sb.tile([P, I // 16], U16, name="note_list")
        col_list = sb.tile([P, G // 16], U16, name="col_list")
        key_scales = sb.tile([P, T], U8, name="key_scales", align_bytes=64)
        key_words = sb.tile([P, T], I32, name="key_words", align_bytes=64)
        worth_pool = sb.tile([P, T], F32, name="worth_pool")
        planes = [sb.tile([P, U], F32, name=f"plane{t}", tag=f"plane{t}") for t in range(PACK)]
        q_raw = [sb.tile([P, PACK, Q], F32, name=f"q_raw{s}") for s in range(2)]
        placed = sb.tile([P, M], F32, name="placed")
        k_scales = sb.tile([P, I], U8, name="k_scales", align_bytes=64)
        ident = sb.tile([P, P], F32, name="ident")

        warm = sb.tile([P, 2], F32, name="warm")
        nc.gpsimd.memset(warm[:, 0:1], 0.0)
        nc.scalar.activation(warm[:, 1:2], warm[:, 0:1], COPY)
        nc.gpsimd.memset(key_scales[SCALE_ROW + BLOCKS :, :].bitcast(I32), 0)
        nc.vector.memset(worth_pool[0:WORTH_ROW, :], 0.0)
        nc.vector.memset(key_scales[0:SCALE_ROW, :].bitcast(I32), 0)
        make_identity(nc, ident[:])
        nc.vector.memset(k_scales[:].bitcast(I32), 0)

        note_rows = notes.rearrange("(p t) u -> p t u", t=PACK)
        scale_rows = keys_scales[0].bitcast(I32)
        nc.sync.dma_start(planes[0][:], note_rows[:, 0, :])
        nc.sync.dma_start(note_list[:], offs2)
        nc.sync.dma_start(tok_list[:], offs)
        nc.sync.dma_start(key_scales[SCALE_ROW : SCALE_ROW + BLOCKS, :].bitcast(I32), scale_rows)
        nc.sync.dma_start(worth_pool[WORTH_ROW : WORTH_ROW + 1, :], worth[0:1, :])
        for t in range(1, PACK):
            nc.sync.dma_start(planes[t][:], note_rows[:, t, :])
        nc.sync.dma_start(q_raw[0][:], query2.rearrange("(p t) q -> p t q", t=PACK))
        nc.sync.dma_start(q_raw[1][:], query.rearrange("(p t) q -> p t q", t=PACK))
        nc.sync.dma_start(key_words[:], keys_words[0].rearrange("p n t -> p (n t)").bitcast(I32))
        nc.sync.dma_start(col_list[:], offs3)

        def half_list(lst, h):
            return lst[:, h * (HALF // 16) : (h + 1) * (HALF // 16)]

        picked = [sb.tile([P, PACK, HALF], BF16, name=f"picked{h}", tag=f"staging{h}") for h in range(2)]

        def gather_note(t, h, on_scalar):
            src = planes[t][:].indirect(half_list(note_list, h))
            if on_scalar:
                nc.scalar.activation(picked[h][:, t, :], src, COPY)
            else:
                nc.vector.tensor_copy(picked[h][:, t, :], src)

        worth_row = sb.tile([P, I], F32, name="worth_row")
        picked_scales = sb.tile([P, I], U8, name="picked_scales", align_bytes=64)

        gather_note(0, 0, False)
        gather_note(0, 1, False)
        nc.vector.tensor_copy(picked_scales[:], key_scales[:].indirect(tok_list[:]))
        for quad in range(4):
            row = SCALE_ROW + 4 * quad
            nc.sync.dma_start(
                k_scales[32 * quad : 32 * quad + 4, :].bitcast(I32), picked_scales[row : row + 4, :].bitcast(I32)
            )
        nc.scalar.activation(worth_row[:], worth_pool[:].indirect(tok_list[:]), COPY)
        gather_note(1, 0, True)
        gather_note(1, 1, True)
        gather_note(2, 0, False)
        gather_note(2, 1, True)
        nc.vector.memset(placed[:], 0.0)
        gather_note(3, 0, False)
        gather_note(3, 1, True)
        old_sb = sb.tile([P, M], F32, name="old_sb", tag="plane3")
        nc.sync.dma_start(old_sb[:], old)

        woven = [sb.tile([P, HALF, PACK], BF16, name=f"woven{h}", align_bytes=64) for h in range(2)]
        n_codes = [sb.tile([P, HALF], U32, name=f"n_codes{h}", align_bytes=64) for h in range(2)]
        n_scales = [sb.tile([P, HALF], U8, name=f"n_scales{h}", align_bytes=64) for h in range(2)]
        nc.vector.tensor_copy(*weave_views(woven[0][:], picked[0][:]))
        nc.vector.tensor_copy(*weave_views(woven[1][:, :WEAVE_SPLIT, :], picked[1][:, :, :WEAVE_SPLIT]))
        nc.scalar.copy(*weave_views(woven[1][:, WEAVE_SPLIT:, :], picked[1][:, :, WEAVE_SPLIT:]))
        for h in range(2):
            nc.vector.quantize_mx(
                out=n_codes[h][:].bitcast(FP8X4),
                scales=n_scales[h][:],
                in_=woven[h][:].rearrange("p c t -> p (c t)"),
            )

        q_woven = sb.tile([P, 2 * Q, PACK], BF16, name="q_woven", align_bytes=64)
        q_codes = sb.tile([P, 2 * Q], U32, name="q_codes", align_bytes=64)
        q_scales = sb.tile([P, 2 * Q], U8, name="q_scales", align_bytes=64)
        for s in range(2):
            dst, src = weave_views(q_woven[:, s * Q : (s + 1) * Q, :], q_raw[s][:])
            nc.scalar.copy(dst, src)
        nc.vector.quantize_mx(
            out=q_codes[:].bitcast(FP8X4), scales=q_scales[:], in_=q_woven[:].rearrange("p c t -> p (c t)")
        )

        turned = ps.tile([P, I // P, P], F32, name="turned")
        spread = ps.tile([P, I], F32, name="spread")
        worth_col = sb.tile([P, I // P], F32, name="worth_col")
        weight = sb.tile([P, I], F32, name="weight", tag="staging1")
        for c in range(I // P):
            nc.tensor.transpose(turned[:, c, :], worth_row[:, c * P : (c + 1) * P], ident[:])
        nc.scalar.activation(worth_col[:], turned[:, :, WORTH_ROW], COPY, scale=2.0)
        for c in range(I // P):
            nc.tensor.transpose(
                spread[:, c * P : (c + 1) * P], worth_col[:, c : c + 1].to_broadcast([P, P]), ident[:]
            )
        nc.scalar.copy(weight[:], spread[:])

        k_codes = [sb.tile([P, n], U32, name=f"k_codes{lo}", align_bytes=64) for lo, n in PIECES]
        scores = [ps.tile([P, n], F32, name=f"scores{lo}") for lo, n in PIECES]
        for (lo, n), bank in zip(PIECES, scores):
            h, at = divmod(lo, HALF)
            nc.tensor.matmul_mx(
                out=bank[:],
                lhsT=q_codes[:, 0:Q].bitcast(FP8X4),
                lhsT_scale=q_scales[:, 0:Q],
                rhs=n_codes[h][:, at : at + n].bitcast(FP8X4),
                rhs_scale=n_scales[h][:, at : at + n],
                start=True,
                stop=False,
            )
        for (lo, n), bank, codes in zip(PIECES, scores, k_codes):
            nc.vector.tensor_copy(
                codes[:], key_words[:].bitcast(U32).indirect(tok_list[:, lo // 16 : (lo + n) // 16])
            )
            nc.tensor.matmul_mx(
                out=bank[:],
                lhsT=q_codes[:, Q : 2 * Q].bitcast(FP8X4),
                lhsT_scale=q_scales[:, Q : 2 * Q],
                rhs=codes[:].bitcast(FP8X4),
                rhs_scale=k_scales[:, lo : lo + n],
                start=False,
                stop=True,
            )

        weighted = [sb.tile([P, n], F32, name=f"weighted{lo}") for lo, n in PIECES]
        sums = sb.tile([P, G], F32, name="sums")
        for (lo, n), bank, ws in zip(PIECES, scores, weighted):
            nc.vector.scalar_tensor_tensor(ws[:], bank[:], 0.0, weight[:, lo : lo + n], ALU.max, ALU.mult)
        for (lo, n), ws in zip(PIECES, weighted):
            nc.vector.tensor_reduce(
                sums[:, lo // RUN : (lo + n) // RUN],
                ws[:].rearrange("p (g j) -> p g j", j=RUN),
                mybir.AxisListType.X,
                ALU.add,
            )
        nc.scalar.activation(placed[:].indirect(col_list[:]), sums[:], COPY)
        for h, queue in enumerate((nc.sync, nc.scalar)):
            cols = slice(h * (M // 2), (h + 1) * (M // 2))
            result = sb.tile([P, M // 2], F32, name=f"result{h}")
            nc.vector.tensor_tensor(result[:], placed[:, cols], old_sb[:, cols], ALU.add)
            queue.dma_start(out[:, cols], result[:])
